import numpy as np
CORES = [1,9,129,137,257,265,385,393]
N = 8
def setup_inputs(rng):
    return {"x": rng.standard_normal((N, 128, 256), dtype=np.float32)}
def reference(x):
    s = np.cumsum(x.astype(np.float64), axis=0)
    return {"y": s.astype(x.dtype)}

@@ -1,0 +1,156 @@
+import concourse.bass as bass
+from concourse.mybir import AluOpType
+
+NQ = 4
+SEND = (2, 3, 6, 7)
+FOLD = (2, 0, 6, 4)
+CABLE = {0: 3, 1: 2}
+
+SCRATCH = {
+    "xs": ("dram", [NQ, 128, 64], "float32"),
+    "ls": ("dram", [NQ, 128, 64], "float32"),
+    "l1": ("dram", [NQ, 128, 64], "float32"),
+    "l2": ("dram", [NQ, 128, 64], "float32"),
+    "hb": ("dram", [4, 128, 64], "float32"),
+}
+SEMAPHORES = ["ld", "st", "snd", "h1", "h2", "r1", "r2", "rs"]
+
+
+def at(h, p, c):
+    return 128 * h + 8 * p + c
+
+
+def rank_program(g, core, T, topo):
+    h, p, c = topo.host(core), topo.chip(core), core % 8
+    if p > 1:
+        return
+    sem = T.sem
+    sent = [0]
+    stored = [0]
+    own, oth, esum, osum = T.hb[0], T.hb[1], T.hb[2], T.hb[3]
+
+    def xfer(srcs, dests, rsem, lo, n):
+        ids = []
+        for d, ap in dests:
+            rid, pid = topo.addr(d, core)
+            ids.append(bass.DstId(rid=rid, pnc=pid))
+        sent[0] += n
+        return bass.RemoteDMATransfer(dst_ids=ids, dma_engine_mask=((1 << n) - 1) << lo, remote_sem=rsem,
+                                      srcs=list(srcs), dsts=[ap for d, ap in dests], alu_op=1 if len(srcs) > 1 else 0)
+
+    def call(transfers):
+        g.remote_dma_fused(transfers, local_sem=sem.snd)
+
+    def finish():
+        if sent[0]:
+            g.wait_ge(sem.snd, sent[0])
+
+    def to_y(src, add):
+        if stored[0]:
+            g.wait_ge(sem.st, stored[0])
+        if add:
+            d = g.dma_start(T.y[:], src, accum_op=AluOpType.add, max_dma_last_dim=8192)
+        else:
+            d = g.dma_start(T.y[:], src)
+        stored[0] += 16
+        d.then_inc(sem.st, 16)
+
+    if c == 1:
+        r = T.rank_of(core)
+        if r != 7:
+            g.dma_start(T.xs[:], T.x[:]).then_inc(sem.ld, 16)
+            g.wait_ge(sem.ld, 16)
+            tr = []
+            for q in range(NQ):
+                s = SEND[q]
+                if r <= 3:
+                    tr.append(xfer([T.xs[q]], [(at(1 - h, p, s), oth)], sem.h1, 2 * q, 2))
+                    tr.append(xfer([T.xs[q]], [(at(h, p, s), own)], sem.h1, 8 + 2 * q, 2))
+                elif r == 4:
+                    tr.append(xfer([T.xs[q]], [(at(3, 0, s), oth)], sem.h1, 2 * q, 2))
+                    tr.append(xfer([T.xs[q]], [(at(2, 0, s), own)], sem.h1, 8 + 2 * q, 2))
+                elif r == 5:
+                    tr.append(xfer([T.xs[q]], [(at(3, 1, 1), T.l1[q])], sem.r1, 2 * q, 2))
+                    tr.append(xfer([T.xs[q]], [(at(2, 1, s), own)], sem.h1, 8 + 2 * q, 2))
+                else:
+                    tr.append(xfer([T.xs[q]], [(at(3, 0, s), own)], sem.h1, 4 * q, 4))
+            call(tr)
+        if r in (0, 1, 4, 5, 7):
+            to_y(T.x[:], False)
+        if r == 1:
+            g.wait_ge(sem.r1, 32)
+            to_y(T.l1[:], True)
+        elif r == 2:
+            g.wait_ge(sem.r1, 16)
+            to_y(T.l1[:], False)
+            g.wait_ge(sem.r2, 32)
+            to_y(T.l2[:], True)
+        elif r == 3:
+            g.wait_ge(sem.rs, 32)
+            to_y(T.ls[:], False)
+        elif r == 5:
+            g.wait_ge(sem.r1, 32)
+            to_y(T.l1[:], True)
+        elif r == 6:
+            g.wait_ge(sem.r1, 32)
+            to_y(T.l1[:], False)
+            g.wait_ge(sem.r2, 32)
+            to_y(T.l2[:], True)
+        elif r == 7:
+            g.wait_ge(sem.r1, 8)
+            to_y(T.l1[:], True)
+            g.wait_ge(sem.r2, 32)
+            to_y(T.l2[:], True)
+        if r >= 4:
+            g.wait_ge(sem.rs, 32)
+            to_y(T.ls[:], True)
+        g.wait_ge(sem.st, stored[0])
+        finish()
+        return
+
+    if h <= 1:
+        def fold_s(srcs, q):
+            tr = [xfer(srcs, [(at(CABLE[h], p, 1), T.ls[q])], sem.rs, 0, 8)]
+            if (h, p) == (1, 1):
+                tr.append(xfer(srcs, [(at(1, 1, 1), T.ls[q])], sem.rs, 8, 8))
+            call(tr)
+
+        if c in SEND:
+            q = SEND.index(c)
+            f = FOLD[q]
+            g.wait_ge(sem.h1, 4)
+            tr = [xfer([own, oth], [(at(h, 1 - p, f), osum)], sem.h2, 0, 8)]
+            if f != c:
+                tr.append(xfer([own, oth], [(at(h, p, f), esum)], sem.h2, 8, 4))
+            if (h, p) == (1, 0):
+                tr.append(xfer([own, oth], [(at(1, 0, 1), T.l1[q])], sem.r1, 12, 4))
+            call(tr)
+            if (h, p) == (0, 0):
+                call([xfer([own], [(at(0, 1, 1), T.l1[q])], sem.r1, 0, 8)])
+            if (h, p) == (1, 1):
+                call([xfer([oth], [(at(1, 0, 1), T.l2[q])], sem.r2, 0, 8)])
+            if f == c:
+                g.wait_ge(sem.h2, 8)
+                fold_s([own, oth, osum], q)
+            finish()
+        elif c in FOLD:
+            q = FOLD.index(c)
+            g.wait_ge(sem.h2, 12)
+            fold_s([esum, osum], q)
+            finish()
+        return
+
+    if c not in SEND or (h, p) == (3, 1):
+        return
+    q = SEND.index(c)
+    if (h, p) == (2, 0):
+        g.wait_ge(sem.h1, 2)
+        call([xfer([own], [(at(2, 1, 1), T.l1[q])], sem.r1, 0, 8)])
+    elif (h, p) == (2, 1):
+        g.wait_ge(sem.h1, 2)
+        call([xfer([own], [(at(3, 0, 1), T.l2[q])], sem.r2, 0, 8)])
+    else:
+        g.wait_ge(sem.h1, 6)
+        call([xfer([own, oth], [(at(3, 1, 1), T.l2[q])], sem.r2, 0, 8),
+              xfer([own, oth], [(at(3, 0, 1), T.l1[q])], sem.r1, 8, 8)])
+    finish()

@@ -66,16 +66,13 @@ def rank_program(g, core, T, topo):
                 if r <= 3:
                     tr.append(xfer([T.xs[q]], [(at(1 - h, p, s), oth)], sem.h1, 2 * q, 2))
                     tr.append(xfer([T.xs[q]], [(at(h, p, s), own)], sem.h1, 8 + 2 * q, 2))
-                elif r == 4:
-                    tr.append(xfer([T.xs[q]], [(at(3, 0, s), oth)], sem.h1, 2 * q, 2))
-                    tr.append(xfer([T.xs[q]], [(at(2, 0, s), own)], sem.h1, 8 + 2 * q, 2))
-                elif r == 5:
-                    tr.append(xfer([T.xs[q]], [(at(3, 1, 1), T.l1[q])], sem.r1, 2 * q, 2))
-                    tr.append(xfer([T.xs[q]], [(at(2, 1, s), own)], sem.h1, 8 + 2 * q, 2))
+                elif r <= 5:
+                    tr.append(xfer([T.xs[q]], [(at(3, p, 1), T.l1[q])], sem.r1, 2 * q, 2))
+                    tr.append(xfer([T.xs[q]], [(at(2, p, s), own)], sem.h1, 8 + 2 * q, 2))
                 else:
-                    tr.append(xfer([T.xs[q]], [(at(3, 0, s), own)], sem.h1, 4 * q, 4))
+                    tr.append(xfer([T.xs[q]], [(at(2, 0, s), oth)], sem.h1, 2 * q, 2))
             call(tr)
-        if r in (0, 1, 4, 5, 7):
+        if r not in (2, 3):
             to_y(T.x[:], False)
         if r == 1:
             g.wait_ge(sem.r1, 32)
@@ -89,17 +86,12 @@ def rank_program(g, core, T, topo):
             g.wait_ge(sem.rs, 32)
             to_y(T.ls[:], False)
         elif r == 5:
-            g.wait_ge(sem.r1, 32)
+            g.wait_ge(sem.r1, 16)
             to_y(T.l1[:], True)
-        elif r == 6:
-            g.wait_ge(sem.r1, 32)
-            to_y(T.l1[:], False)
-            g.wait_ge(sem.r2, 32)
-            to_y(T.l2[:], True)
-        elif r == 7:
+        elif r in (6, 7):
             g.wait_ge(sem.r1, 8)
             to_y(T.l1[:], True)
-            g.wait_ge(sem.r2, 32)
+            g.wait_ge(sem.r2, 32 if r == 6 else 16)
             to_y(T.l2[:], True)
         if r >= 4:
             g.wait_ge(sem.rs, 32)
@@ -140,17 +132,14 @@ def rank_program(g, core, T, topo):
             finish()
         return
 
-    if c not in SEND or (h, p) == (3, 1):
+    if c not in SEND or h == 3:
         return
     q = SEND.index(c)
-    if (h, p) == (2, 0):
-        g.wait_ge(sem.h1, 2)
-        call([xfer([own], [(at(2, 1, 1), T.l1[q])], sem.r1, 0, 8)])
-    elif (h, p) == (2, 1):
+    if p == 0:
+        g.wait_ge(sem.h1, 4)
+        call([xfer([own, oth], [(at(3, 1, 1), T.l2[q])], sem.r2, 0, 4),
+              xfer([own], [(at(2, 1, 1), T.l1[q])], sem.r1, 4, 4)])
+    else:
         g.wait_ge(sem.h1, 2)
         call([xfer([own], [(at(3, 0, 1), T.l2[q])], sem.r2, 0, 8)])
-    else:
-        g.wait_ge(sem.h1, 6)
-        call([xfer([own, oth], [(at(3, 1, 1), T.l2[q])], sem.r2, 0, 8),
-              xfer([own, oth], [(at(3, 0, 1), T.l1[q])], sem.r1, 8, 8)])
     finish()

@@ -13,7 +13,7 @@ SCRATCH = {
     "l2": ("dram", [NQ, 128, 64], "float32"),
     "hb": ("dram", [4, 128, 64], "float32"),
 }
-SEMAPHORES = ["ld", "st", "snd", "h1", "h2", "r1", "r2", "rs"]
+SEMAPHORES = ["ld", "st", "snd", "h1", "h2", "r1", "r2", "r3", "rs"]
 
 
 def at(h, p, c):
@@ -27,7 +27,8 @@ def rank_program(g, core, T, topo):
     sem = T.sem
     sent = [0]
     stored = [0]
-    own, oth, esum, osum = T.hb[0], T.hb[1], T.hb[2], T.hb[3]
+    hb = [T.hb[0], T.hb[1], T.hb[2], T.hb[3]]
+    own, oth, esum, osum = hb
 
     def xfer(srcs, dests, rsem, lo, n):
         ids = []
@@ -45,13 +46,15 @@ def rank_program(g, core, T, topo):
         if sent[0]:
             g.wait_ge(sem.snd, sent[0])
 
-    def to_y(src, add):
+    def to_y(src, add, dst=None):
+        if dst is None:
+            dst = T.y[:]
         if stored[0]:
             g.wait_ge(sem.st, stored[0])
         if add:
-            d = g.dma_start(T.y[:], src, accum_op=AluOpType.add, max_dma_last_dim=8192)
+            d = g.dma_start(dst, src, accum_op=AluOpType.add, max_dma_last_dim=8192)
         else:
-            d = g.dma_start(T.y[:], src)
+            d = g.dma_start(dst, src)
         stored[0] += 16
         d.then_inc(sem.st, 16)
 
@@ -60,28 +63,31 @@ def rank_program(g, core, T, topo):
         if r != 7:
             g.dma_start(T.xs[:], T.x[:]).then_inc(sem.ld, 16)
             g.wait_ge(sem.ld, 16)
-            tr = []
+            far, near = [], []
             for q in range(NQ):
                 s = SEND[q]
                 if r <= 3:
-                    tr.append(xfer([T.xs[q]], [(at(1 - h, p, s), oth)], sem.h1, 2 * q, 2))
-                    tr.append(xfer([T.xs[q]], [(at(h, p, s), own)], sem.h1, 8 + 2 * q, 2))
+                    if q < 2:
+                        far.append(xfer([T.xs[q]], [(at(1 - h, p, s), oth)], sem.h1, 4 * q, 4))
+                    near.append(xfer([T.xs[q]], [(at(h, p, s), own)], sem.h1, 8 + 2 * q, 2))
                 elif r <= 5:
-                    tr.append(xfer([T.xs[q]], [(at(3, p, 1), T.l1[q])], sem.r1, 2 * q, 2))
-                    tr.append(xfer([T.xs[q]], [(at(2, p, s), own)], sem.h1, 8 + 2 * q, 2))
+                    far.append(xfer([T.xs[q]], [(at(3, p, 1), T.l1[q])], sem.r1, 2 * q, 2))
+                    near.append(xfer([T.xs[q]], [(at(2, p, s), own)], sem.h1, 8 + 2 * q, 2))
                 else:
-                    tr.append(xfer([T.xs[q]], [(at(2, 0, s), oth)], sem.h1, 2 * q, 2))
-            call(tr)
-        if r not in (2, 3):
+                    far.append(xfer([T.xs[q]], [(at(2, 0, s), oth)], sem.h1, 2 * q, 2))
+            call(far + near)
+        if r != 3:
             to_y(T.x[:], False)
         if r == 1:
             g.wait_ge(sem.r1, 32)
             to_y(T.l1[:], True)
         elif r == 2:
-            g.wait_ge(sem.r1, 16)
-            to_y(T.l1[:], False)
-            g.wait_ge(sem.r2, 32)
-            to_y(T.l2[:], True)
+            g.wait_ge(sem.r1, 8)
+            to_y(T.l1[0:2], True, T.y[0:64, :])
+            g.wait_ge(sem.r2, 16)
+            to_y(T.l2[0:2], True, T.y[0:64, :])
+            g.wait_ge(sem.r3, 16)
+            to_y(T.l1[2:4], True, T.y[64:128, :])
         elif r == 3:
             g.wait_ge(sem.rs, 32)
             to_y(T.ls[:], False)
@@ -105,17 +111,21 @@ def rank_program(g, core, T, topo):
             tr = [xfer(srcs, [(at(CABLE[h], p, 1), T.ls[q])], sem.rs, 0, 8)]
             if (h, p) == (1, 1):
                 tr.append(xfer(srcs, [(at(1, 1, 1), T.ls[q])], sem.rs, 8, 8))
+            elif (h, p) == (0, 1) and q >= 2:
+                tr.append(xfer([hb[2]], [(at(0, 1, 1), T.l1[q])], sem.r1, 8, 8))
+            elif (h, p) == (1, 0) and q >= 2:
+                tr.append(xfer([hb[1], hb[3]], [(at(1, 0, 1), T.l1[q])], sem.r3, 8, 8))
             call(tr)
 
-        if c in SEND:
+        if c in (2, 3):
             q = SEND.index(c)
             f = FOLD[q]
-            g.wait_ge(sem.h1, 4)
+            g.wait_ge(sem.h1, 6)
             tr = [xfer([own, oth], [(at(h, 1 - p, f), osum)], sem.h2, 0, 8)]
             if f != c:
                 tr.append(xfer([own, oth], [(at(h, p, f), esum)], sem.h2, 8, 4))
             if (h, p) == (1, 0):
-                tr.append(xfer([own, oth], [(at(1, 0, 1), T.l1[q])], sem.r1, 12, 4))
+                tr.append(xfer([oth], [(at(1, 0, 1), T.l1[q])], sem.r1, 12, 4))
             call(tr)
             if (h, p) == (0, 0):
                 call([xfer([own], [(at(0, 1, 1), T.l1[q])], sem.r1, 0, 8)])
@@ -124,12 +134,26 @@ def rank_program(g, core, T, topo):
             if f == c:
                 g.wait_ge(sem.h2, 8)
                 fold_s([own, oth, osum], q)
-            finish()
-        elif c in FOLD:
-            q = FOLD.index(c)
+        elif c == 0:
             g.wait_ge(sem.h2, 12)
-            fold_s([esum, osum], q)
-            finish()
+            fold_s([esum, osum], 1)
+        elif c in (6, 7):
+            q = SEND.index(c)
+            f = FOLD[q]
+            g.wait_ge(sem.h1, 2)
+            tr = [xfer([own], [(at(1 - h, 1 - p, f), hb[3]),
+                               (at(1 - h, p, f), hb[1]),
+                               (at(h, 1 - p, f), hb[2])], sem.h2, 0, 8)]
+            if f != c:
+                tr.append(xfer([own], [(at(h, p, f), hb[0])], sem.h2, 8, 8))
+            call(tr)
+            if f == c:
+                g.wait_ge(sem.h2, 24)
+                fold_s(hb, q)
+        elif c == 4:
+            g.wait_ge(sem.h2, 32)
+            fold_s(hb, 3)
+        finish()
         return
 
     if c not in SEND or h == 3:

@@ -13,7 +13,7 @@ SCRATCH = {
     "l2": ("dram", [NQ, 128, 64], "float32"),
     "hb": ("dram", [4, 128, 64], "float32"),
 }
-SEMAPHORES = ["ld", "st", "snd", "h1", "h2", "r1", "r2", "r3", "rs"]
+SEMAPHORES = ["ld", "st", "st2", "snd", "h1", "h2", "r1", "r2", "r3", "rs"]
 
 
 def at(h, p, c):
@@ -76,18 +76,21 @@ def rank_program(g, core, T, topo):
                 else:
                     far.append(xfer([T.xs[q]], [(at(2, 0, s), oth)], sem.h1, 2 * q, 2))
             call(far + near)
-        if r != 3:
+            if r <= 3:
+                call([xfer([T.xs[q]], [(at(1 - h, p, FOLD[q]), hb[1])], sem.h2, 4 * (q - 2), 4) for q in (2, 3)])
+        if r not in (2, 3):
             to_y(T.x[:], False)
         if r == 1:
             g.wait_ge(sem.r1, 32)
             to_y(T.l1[:], True)
         elif r == 2:
             g.wait_ge(sem.r1, 8)
-            to_y(T.l1[0:2], True, T.y[0:64, :])
+            to_y(T.l1[0:2], False, T.y[0:64, :])
             g.wait_ge(sem.r2, 16)
             to_y(T.l2[0:2], True, T.y[0:64, :])
             g.wait_ge(sem.r3, 16)
-            to_y(T.l1[2:4], True, T.y[64:128, :])
+            g.dma_start(T.y[64:128, :], T.l1[2:4]).then_inc(sem.st2, 16)
+            g.wait_ge(sem.st2, 16)
         elif r == 3:
             g.wait_ge(sem.rs, 32)
             to_y(T.ls[:], False)
@@ -114,7 +117,7 @@ def rank_program(g, core, T, topo):
             elif (h, p) == (0, 1) and q >= 2:
                 tr.append(xfer([hb[2]], [(at(0, 1, 1), T.l1[q])], sem.r1, 8, 8))
             elif (h, p) == (1, 0) and q >= 2:
-                tr.append(xfer([hb[1], hb[3]], [(at(1, 0, 1), T.l1[q])], sem.r3, 8, 8))
+                tr.append(xfer([hb[0], hb[1], hb[3]], [(at(1, 0, 1), T.l1[q])], sem.r3, 8, 8))
             call(tr)
 
         if c in (2, 3):
@@ -125,7 +128,7 @@ def rank_program(g, core, T, topo):
             if f != c:
                 tr.append(xfer([own, oth], [(at(h, p, f), esum)], sem.h2, 8, 4))
             if (h, p) == (1, 0):
-                tr.append(xfer([oth], [(at(1, 0, 1), T.l1[q])], sem.r1, 12, 4))
+                tr.append(xfer([own, oth], [(at(1, 0, 1), T.l1[q])], sem.r1, 12, 4))
             call(tr)
             if (h, p) == (0, 0):
                 call([xfer([own], [(at(0, 1, 1), T.l1[q])], sem.r1, 0, 8)])
@@ -142,16 +145,15 @@ def rank_program(g, core, T, topo):
             f = FOLD[q]
             g.wait_ge(sem.h1, 2)
             tr = [xfer([own], [(at(1 - h, 1 - p, f), hb[3]),
-                               (at(1 - h, p, f), hb[1]),
                                (at(h, 1 - p, f), hb[2])], sem.h2, 0, 8)]
             if f != c:
                 tr.append(xfer([own], [(at(h, p, f), hb[0])], sem.h2, 8, 8))
             call(tr)
             if f == c:
-                g.wait_ge(sem.h2, 24)
+                g.wait_ge(sem.h2, 20)
                 fold_s(hb, q)
         elif c == 4:
-            g.wait_ge(sem.h2, 32)
+            g.wait_ge(sem.h2, 28)
             fold_s(hb, 3)
         finish()
         return

import concourse.bass as bass
from concourse.mybir import AluOpType

NQ = 4
SEND = (2, 3, 6, 7)
FOLD = (2, 0, 6, 4)
CABLE = {0: 3, 1: 2}

SCRATCH = {
    "xs": ("dram", [NQ, 128, 64], "float32"),
    "ls": ("dram", [NQ, 128, 64], "float32"),
    "l1": ("dram", [NQ, 128, 64], "float32"),
    "l2": ("dram", [NQ, 128, 64], "float32"),
    "hb": ("dram", [4, 128, 64], "float32"),
}
SEMAPHORES = ["ld", "st", "st2", "snd", "h1", "h2", "r1", "r2", "r3", "rs"]


def at(h, p, c):
    return 128 * h + 8 * p + c


def rank_program(g, core, T, topo):
    h, p, c = topo.host(core), topo.chip(core), core % 8
    if p > 1:
        return
    sem = T.sem
    sent = [0]
    stored = [0]
    hb = [T.hb[0], T.hb[1], T.hb[2], T.hb[3]]
    own, oth, esum, osum = hb

    def xfer(srcs, dests, rsem, lo, n):
        ids = []
        for d, ap in dests:
            rid, pid = topo.addr(d, core)
            ids.append(bass.DstId(rid=rid, pnc=pid))
        sent[0] += n
        return bass.RemoteDMATransfer(dst_ids=ids, dma_engine_mask=((1 << n) - 1) << lo, remote_sem=rsem,
                                      srcs=list(srcs), dsts=[ap for d, ap in dests], alu_op=1 if len(srcs) > 1 else 0)

    def call(transfers):
        g.remote_dma_fused(transfers, local_sem=sem.snd)

    def finish():
        if sent[0]:
            g.wait_ge(sem.snd, sent[0])

    def to_y(src, add, dst=None):
        if dst is None:
            dst = T.y[:]
        if stored[0]:
            g.wait_ge(sem.st, stored[0])
        if add:
            d = g.dma_start(dst, src, accum_op=AluOpType.add, max_dma_last_dim=8192)
        else:
            d = g.dma_start(dst, src)
        stored[0] += 16
        d.then_inc(sem.st, 16)

    if c == 1:
        r = T.rank_of(core)
        if r != 7:
            g.dma_start(T.xs[:], T.x[:]).then_inc(sem.ld, 16)
            g.wait_ge(sem.ld, 16)
            far, near = [], []
            for q in range(NQ):
                s = SEND[q]
                if r <= 3:
                    if q < 2:
                        far.append(xfer([T.xs[q]], [(at(1 - h, p, s), oth)], sem.h1, 4 * q, 4))
                    near.append(xfer([T.xs[q]], [(at(h, p, s), own)], sem.h1, 8 + 2 * q, 2))
                elif r <= 5:
                    far.append(xfer([T.xs[q]], [(at(3, p, 1), T.l1[q])], sem.r1, 2 * q, 2))
                    near.append(xfer([T.xs[q]], [(at(2, p, s), own)], sem.h1, 8 + 2 * q, 2))
                else:
                    far.append(xfer([T.xs[q]], [(at(2, 0, s), oth)], sem.h1, 2 * q, 2))
            call(far + near)
            if r <= 3:
                call([xfer([T.xs[q]], [(at(1 - h, p, FOLD[q]), hb[1])], sem.h2, 4 * (q - 2), 4) for q in (2, 3)])
        if r not in (2, 3):
            to_y(T.x[:], False)
        if r == 1:
            g.wait_ge(sem.r1, 32)
            to_y(T.l1[:], True)
        elif r == 2:
            g.wait_ge(sem.r1, 8)
            to_y(T.l1[0:2], False, T.y[0:64, :])
            g.wait_ge(sem.r2, 16)
            to_y(T.l2[0:2], True, T.y[0:64, :])
            g.wait_ge(sem.r3, 16)
            g.dma_start(T.y[64:128, :], T.l1[2:4]).then_inc(sem.st2, 16)
            g.wait_ge(sem.st2, 16)
        elif r == 3:
            g.wait_ge(sem.rs, 32)
            to_y(T.ls[:], False)
        elif r == 5:
            g.wait_ge(sem.r1, 16)
            to_y(T.l1[:], True)
        elif r in (6, 7):
            g.wait_ge(sem.r1, 8)
            to_y(T.l1[:], True)
            g.wait_ge(sem.r2, 32 if r == 6 else 16)
            to_y(T.l2[:], True)
        if r >= 4:
            g.wait_ge(sem.rs, 32)
            to_y(T.ls[:], True)
        g.wait_ge(sem.st, stored[0])
        finish()
        return

    if h <= 1:
        def fold_s(srcs, q):
            tr = [xfer(srcs, [(at(CABLE[h], p, 1), T.ls[q])], sem.rs, 0, 8)]
            if (h, p) == (1, 1):
                tr.append(xfer(srcs, [(at(1, 1, 1), T.ls[q])], sem.rs, 8, 8))
            elif (h, p) == (0, 1) and q >= 2:
                tr.append(xfer([hb[2]], [(at(0, 1, 1), T.l1[q])], sem.r1, 8, 8))
            elif (h, p) == (1, 0) and q >= 2:
                tr.append(xfer([hb[0], hb[1], hb[3]], [(at(1, 0, 1), T.l1[q])], sem.r3, 8, 8))
            call(tr)

        if c in (2, 3):
            q = SEND.index(c)
            f = FOLD[q]
            g.wait_ge(sem.h1, 6)
            tr = [xfer([own, oth], [(at(h, 1 - p, f), osum)], sem.h2, 0, 8)]
            if f != c:
                tr.append(xfer([own, oth], [(at(h, p, f), esum)], sem.h2, 8, 4))
            if (h, p) == (1, 0):
                tr.append(xfer([own, oth], [(at(1, 0, 1), T.l1[q])], sem.r1, 12, 4))
            call(tr)
            if (h, p) == (0, 0):
                call([xfer([own], [(at(0, 1, 1), T.l1[q])], sem.r1, 0, 8)])
            if (h, p) == (1, 1):
                call([xfer([oth], [(at(1, 0, 1), T.l2[q])], sem.r2, 0, 8)])
            if f == c:
                g.wait_ge(sem.h2, 8)
                fold_s([own, oth, osum], q)
        elif c == 0:
            g.wait_ge(sem.h2, 12)
            fold_s([esum, osum], 1)
        elif c in (6, 7):
            q = SEND.index(c)
            f = FOLD[q]
            g.wait_ge(sem.h1, 2)
            tr = [xfer([own], [(at(1 - h, 1 - p, f), hb[3]),
                               (at(h, 1 - p, f), hb[2])], sem.h2, 0, 8)]
            if f != c:
                tr.append(xfer([own], [(at(h, p, f), hb[0])], sem.h2, 8, 8))
            call(tr)
            if f == c:
                g.wait_ge(sem.h2, 20)
                fold_s(hb, q)
        elif c == 4:
            g.wait_ge(sem.h2, 28)
            fold_s(hb, 3)
        finish()
        return

    if c not in SEND or h == 3:
        return
    q = SEND.index(c)
    if p == 0:
        g.wait_ge(sem.h1, 4)
        call([xfer([own, oth], [(at(3, 1, 1), T.l2[q])], sem.r2, 0, 4),
              xfer([own], [(at(2, 1, 1), T.l1[q])], sem.r1, 4, 4)])
    else:
        g.wait_ge(sem.h1, 2)
        call([xfer([own], [(at(3, 0, 1), T.l2[q])], sem.r2, 0, 8)])
    finish()
